import numpy as np
import ml_dtypes


def mxq(x, axis, fmt="e4m3"):
    dtype, down = {"e4m3": (ml_dtypes.float8_e4m3fn, 7), "e5m2": (ml_dtypes.float8_e5m2, 14)}[fmt]
    v = np.moveaxis(np.asarray(x, np.float32).astype(ml_dtypes.bfloat16).astype(np.float64), axis, -1)
    blocks = v.reshape(v.shape[:-1] + (-1, 32))
    amax = np.abs(blocks).max(-1, keepdims=True)
    byte = np.maximum(np.where(amax > 0, np.frexp(amax)[1] - 1 + 127, 0) - down, 1)
    scale = np.exp2(byte - 127.0)
    codes = (blocks / scale).astype(np.float32).astype(dtype).astype(np.float64)
    return np.moveaxis((codes * scale).reshape(v.shape), -1, axis)


WIDE = False


def mx_kscale(k):
    if not WIDE:
        return np.ones(k)
    levels = np.array([10, -10, 5, -5, 0])
    if k % 512:
        return np.exp2(np.random.permutation(np.resize(levels, k // 32))).repeat(32)
    a = np.empty((k // 512, 16))
    for p in range(k // 512):
        a[p, :8] = np.random.permutation(np.resize(levels, 8))
        for g in range(8):
            far = levels[np.abs(levels - a[p, g]) >= 10]
            a[p, g + 8] = far[np.random.randint(len(far))]
    return np.exp2(a.ravel()).repeat(32)


def f64(x):
    return np.asarray(x).astype(np.float64)


def striped(idx):
    return np.tile(np.asarray(idx).reshape(-1, 16).T, (8, 1)).astype(np.uint16)


def unstriped(offs):
    return offs[:16].T.reshape(-1).astype(np.int64)


E2M1 = np.array([0.0, 0.5, 1.0, 1.5, 2.0, 3.0, 4.0, 6.0, -0.0, -0.5, -1.0, -1.5, -2.0, -3.0, -4.0, -6.0])


def pack_weight(w, fmt):
    k, n = w.shape
    w = f64(np.asarray(w, np.float32).astype(ml_dtypes.bfloat16)).reshape(k // 32, 32, n)
    amax = np.abs(w).max(1)
    if fmt == "e4m3":
        byte = np.frexp(amax)[1] - 1 + 127 - 7
    else:
        mant, ex = np.frexp(amax / 6.0)
        byte = np.where(mant > 0.5, ex, ex - 1) + 127
    byte = np.clip(np.where(amax > 0, byte, 1), 1, 254)
    scaled = (w * np.exp2(127.0 - byte)[:, None, :]).reshape(k, n).astype(np.float32)
    by_word = np.ascontiguousarray(scaled.reshape(k // 512, 128, 4, n).transpose(0, 1, 3, 2))
    if fmt == "e4m3":
        words = by_word.astype(ml_dtypes.float8_e4m3fn).view(np.uint8)
    else:
        c = by_word.astype(ml_dtypes.float4_e2m1fn).view(np.uint8) & 0xF
        words = (c[..., 0::2] | (c[..., 1::2] << 4)).reshape(k // 512, 128, 2 * n)
    return np.ascontiguousarray(words), np.ascontiguousarray(byte.astype(np.uint8).reshape(k // 512, 16, n))


def unpack_weight(words, scales, fmt):
    g, _, n = scales.shape
    words = np.ascontiguousarray(words).reshape(g, 128, n, -1)
    if fmt == "e4m3":
        vals = words.view(ml_dtypes.float8_e4m3fn).astype(np.float64)
    else:
        nib = np.empty((g, 128, n, 4), np.uint8)
        nib[..., 0::2] = words & 0xF
        nib[..., 1::2] = words >> 4
        vals = E2M1[nib]
    vals = vals * np.repeat(np.exp2(scales.astype(np.float64) - 127.0), 8, axis=1)[..., None]
    return vals.transpose(0, 1, 3, 2).reshape(g * 512, n)


D, E, T, I, Q = 512, 512, 2048, 512, 128


def setup_inputs():
    n = np.random.standard_normal
    idx = np.random.permutation(T)[:I]
    fd = mx_kscale(D)
    fe = mx_kscale(E)
    keysp = pack_weight(n((D, T)) / fd[:, None], "e2m1")
    valsp = pack_weight(n((E, T)) / fe[:, None], "e2m1")
    return {
        "query": (n((D, Q)) * 1.0 / np.sqrt(D) * fd[:, None]).astype(np.float32),
        "keys_words": keysp[0],
        "keys_scales": keysp[1],
        "floor": (np.random.uniform(0.05, 0.3, (Q, 1))).astype(np.float32),
        "reserve": (np.random.uniform(20.0, 100.0, (Q, 1))).astype(np.float32),
        "gout": (n((E, Q)) * 1 / np.sqrt(E) * fe[:, None]).astype(np.float32),
        "vals_words": valsp[0],
        "vals_scales": valsp[1],
        "base": (0.5 * n((Q, I))).astype(np.float32),
        "offs": striped(idx),
    }


def reference(query, keys_words, keys_scales, floor, reserve, gout, vals_words, vals_scales, base, offs):
    idx = unstriped(offs)
    keysu = unpack_weight(keys_words, keys_scales, "e2m1")
    valsu = unpack_weight(vals_words, vals_scales, "e2m1")
    queryq = mxq(f64(query), 0, "e4m3")
    keysidxg = keysu[:, idx]
    a = queryq.T @ keysidxg
    p = np.square(a) + f64(floor)
    z = np.sum(p, axis=1, keepdims=True) + f64(reserve)
    goutq = mxq(f64(gout), 0, "e4m3")
    valsidxg = valsu[:, idx]
    c0 = goutq.T @ valsidxg
    dz = np.sum(c0 * p / np.square(z) * (-1.0), axis=1, keepdims=True)
    dp = c0 / z + dz
    da = dp * a * 2.0
    hda = da * 512.0 * 2.0 * 512.0
    hdp = hda * 2.0 * a
    hdz = np.sum(hdp, axis=1, keepdims=True)
    hz = np.sum(hdp * c0 / np.square(z) * (-1.0), axis=1, keepdims=True) + np.sum(hdz * (-1.0) * c0 * p / np.square(np.square(z)) * (-1.0), axis=1, keepdims=True) * z * 2.0
    hp = hdz * (-1.0) / np.square(z) * c0 + hz
    ha = hda * 2.0 * dp + hp * a * 2.0
    y = ha + f64(base)
    return y

@@ -1,0 +1,193 @@
+import math
+from contextlib import ExitStack
+
+import concourse.mybir as mybir
+
+D, E, T, SLOTS, Q = 512, 512, 2048, 512, 128
+P = 128
+PACK = 4
+HALF = SLOTS // 2
+LIST_ROWS = 16
+PENALTY_GAIN = 4.0 * 512.0 * 2.0 * 512.0
+
+FLOPS = 2 * Q * SLOTS * (D + E)
+
+F32 = mybir.dt.float32
+BF16 = mybir.dt.bfloat16
+I32 = mybir.dt.int32
+U32 = mybir.dt.uint32
+U16 = mybir.dt.uint16
+U8 = mybir.dt.uint8
+FP8X4 = mybir.dt.float8_e4m3fn_x4
+FP4X4 = mybir.dt.float4_e2m1fn_x4
+MULT = mybir.AluOpType.mult
+ADD = mybir.AluOpType.add
+COPY = mybir.ActivationFunctionType.Copy
+IDENT = mybir.ActivationFunctionType.Identity
+SQUARE = mybir.ActivationFunctionType.Square
+
+
+def load_scale_rows(queue, plane, scales):
+    for quad in range(4):
+        queue.dma_start(
+            out=plane[32 * quad : 32 * quad + 4, :].bitcast(I32),
+            in_=scales[0, 4 * quad : 4 * quad + 4, :].bitcast(I32),
+        )
+
+
+def interleave(nc, grouped, raw):
+    nc.scalar.copy(
+        out=grouped[:].rearrange("p (c i t) -> p c t i", i=4, t=PACK),
+        in_=raw[:].rearrange("p t (c i) -> p c t i", i=4),
+    )
+
+
+def tile_attend_gpsquareshares_kernel(
+    tc, query, keys_words, keys_scales, floor, reserve, gout, vals_words, vals_scales, base, offs, out
+):
+    nc = tc.nc
+    with ExitStack() as ctx:
+        sb = ctx.enter_context(tc.tile_pool(name="sb", bufs=1))
+        ps = ctx.enter_context(tc.psum_pool(name="ps", bufs=1))
+
+        offsets = sb.tile([P, SLOTS // LIST_ROWS], U16, name="offsets")
+        key_plane = sb.tile([P, T], U8, name="key_plane", align_bytes=64)
+        val_plane = sb.tile([P, T], U8, name="val_plane", align_bytes=64)
+        key_pool = sb.tile([P, T], U16, name="key_pool", align_bytes=64)
+        late = ctx.enter_context(tc.tile_pool(name="late", bufs=1))
+        seed = late.tile([P, 1552], F32, name="seed", offset=0)
+        coef_u = sb.tile([P, 5], F32, name="coef_u")
+
+        nc.vector.memset(key_plane[:].bitcast(I32), 0)
+        nc.vector.memset(seed[:, 0:1], 1.0)
+        nc.vector.memset(seed[:, 1:5], 0.0)
+        nc.vector.tensor_copy(coef_u[:], seed[:, 0:5])
+        nc.vector.memset(val_plane[:].bitcast(I32), 0)
+
+        q_raw = late.tile([P, PACK, Q], F32, name="q_raw", offset=0)
+        val_pool = late.tile([P, T], U16, name="val_pool", offset=2048)
+        g_raw = late.tile([P, PACK, Q], F32, name="g_raw", offset=6144)
+        floor_sb = sb.tile([P, 1], F32, name="floor_sb")
+        reserve_sb = sb.tile([P, 1], F32, name="reserve_sb")
+
+        nc.sync.dma_start(offsets[:], offs)
+        nc.sync.dma_start(out=key_pool[:].bitcast(I32), in_=keys_words[0].bitcast(I32))
+        load_scale_rows(nc.sync, key_plane, keys_scales)
+        nc.sync.dma_start(out=q_raw[:], in_=query.rearrange("(p t) q -> p t q", t=PACK))
+        nc.sync.dma_start(out=val_pool[:].bitcast(I32), in_=vals_words[0].bitcast(I32))
+        load_scale_rows(nc.sync, val_plane, vals_scales)
+        nc.sync.dma_start(out=g_raw[:], in_=gout.rearrange("(p t) q -> p t q", t=PACK))
+        nc.gpsimd.dma_start(out=floor_sb[:], in_=floor)
+        nc.gpsimd.dma_start(out=reserve_sb[:], in_=reserve)
+
+        order = ctx.enter_context(tc.tile_pool(name="order", bufs=1))
+        q_grouped = order.tile([P, Q * PACK], BF16, name="q_grouped", tag="words0", align_bytes=64)
+        g_grouped = order.tile([P, Q * PACK], BF16, name="g_grouped", tag="g_then_words", align_bytes=64)
+        interleave(nc, q_grouped, q_raw)
+        interleave(nc, g_grouped, g_raw)
+
+        base_sb = late.tile([P, SLOTS], F32, name="base_sb", offset=0)
+        nc.sync.dma_start(out=base_sb[:], in_=base)
+
+        raw_cols = sb.tile([P, 7], F32, name="raw_cols")
+        cols = sb.tile([P, 10], F32, name="cols")
+        sums = sb.tile([P, 2, 5], F32, name="sums")
+        nc.vector.memset(raw_cols[:, 5:6], 0.0)
+        nc.vector.memset(sums[:, 1, 2:4], 1.0)
+
+        rest = sb.tile([P, 1], F32, name="rest")
+        nc.scalar.activation(rest[:], floor_sb[:], IDENT, bias=reserve_sb[:], scale=float(SLOTS))
+        nc.scalar.activation(raw_cols[:, 3:4], floor_sb[:], COPY)
+        nc.scalar.activation(raw_cols[:, 4:5], floor_sb[:], COPY, scale=2.0)
+        nc.scalar.activation(raw_cols[:, 6:7], floor_sb[:], COPY, scale=-1.0)
+        nc.scalar.activation(raw_cols[:, 0:1], rest[:], COPY, scale=2.0)
+        nc.scalar.activation(raw_cols[:, 2:3], rest[:], COPY, scale=-1.0)
+
+        key_scale = sb.tile([P, SLOTS], U8, name="key_scale", align_bytes=64)
+        key_words = sb.tile([P, SLOTS], U16, name="key_words", align_bytes=64)
+        nc.vector.tensor_copy(key_words[:], key_pool[:].indirect(offsets[:]))
+        nc.vector.tensor_copy(key_scale[:], key_plane[:].indirect(offsets[:]))
+        q_codes = sb.tile([P, Q], U32, name="q_codes", align_bytes=64)
+        q_scale = sb.tile([P, Q], U8, name="q_scale", align_bytes=64)
+        nc.vector.quantize_mx(out=q_codes[:].bitcast(FP8X4), scales=q_scale[:], in_=q_grouped[:])
+
+        score = ps.tile([P, SLOTS], F32, name="score")
+        nc.tensor.matmul_mx(
+            out=score[:], lhsT=q_codes[:].bitcast(FP8X4), lhsT_scale=q_scale[:],
+            rhs=key_words[:].bitcast(FP4X4), rhs_scale=key_scale[:], start=True, stop=True,
+        )
+        sq = sb.tile([P, SLOTS], F32, name="sq")
+        nc.scalar.activation(sq[:], score[:], SQUARE, accum_out=raw_cols[:, 1:2])
+        total = order.tile([P, 1], F32, name="total", tag="total_then_scale", align_bytes=64)
+        nc.scalar.activation(total[:], raw_cols[:, 1:2], IDENT, bias=rest[:])
+
+        g_codes = sb.tile([P, Q], U32, name="g_codes", align_bytes=64)
+        g_scale = sb.tile([P, Q], U8, name="g_scale", align_bytes=64)
+        nc.vector.quantize_mx(out=g_codes[:].bitcast(FP8X4), scales=g_scale[:], in_=g_grouped[:])
+
+        inv = sb.tile([P, 1], F32, name="inv")
+        nc.vector.reciprocal(inv[:], total[:])
+        nc.scalar.activation(cols[:, 0:7], raw_cols[:], COPY, scale=inv[:])
+        prtau = sb.tile([P, 1], F32, name="prtau")
+        sigma2 = sb.tile([P, 1], F32, name="sigma2")
+        gain = sb.tile([P, 1], F32, name="gain")
+        nc.scalar.activation(prtau[:], cols[:, 3:4], IDENT, bias=cols[:, 4:5], scale=cols[:, 1:2])
+        nc.scalar.activation(sigma2[:], cols[:, 1:2], SQUARE)
+        nc.scalar.activation(cols[:, 9:10], cols[:, 2:3], COPY, scale=cols[:, 3:4])
+        nc.scalar.activation(coef_u[:, 4:5], cols[:, 2:3], COPY, bias=-1.0)
+        nc.scalar.activation(cols[:, 7:9], cols[:, 0:2], COPY, scale=prtau[:])
+        nc.scalar.activation(coef_u[:, 2:3], sigma2[:], COPY, bias=3.0, scale=-1.0)
+        nc.scalar.activation(gain[:], inv[:], SQUARE, scale=math.sqrt(PENALTY_GAIN))
+        coef_c = cols[:, 5:10]
+
+        halves = [slice(h * HALF, (h + 1) * HALF) for h in range(2)]
+        c_sb = sb.tile([P, SLOTS], F32, name="c_sb")
+        c_ps = []
+        c_sum = []
+        for h in range(2):
+            val_words = order.tile([P, HALF], U16, name="val_words%d" % h, tag=("words0", "g_then_words")[h], align_bytes=64)
+            lo = h * HALF // LIST_ROWS
+            nc.vector.tensor_copy(val_words[:], val_pool[:].indirect(offsets[:, lo : lo + HALF // LIST_ROWS]))
+            val_scale = order.tile([P, HALF], U8, name="val_scale%d" % h, tag=("scale0", "total_then_scale")[h], align_bytes=64)
+            nc.vector.tensor_copy(val_scale[:], val_plane[:].indirect(offsets[:, lo : lo + HALF // LIST_ROWS]))
+            bank = ps.tile([P, HALF], F32, name="c_ps%d" % h)
+            nc.tensor.matmul_mx(
+                out=bank[:], lhsT=g_codes[:].bitcast(FP8X4), lhsT_scale=g_scale[:],
+                rhs=val_words[:].bitcast(FP4X4), rhs_scale=val_scale[:], start=True, stop=True,
+            )
+            part = sb.tile([P, 1], F32, name="c_sum%d" % h)
+            nc.scalar.activation(c_sb[:, halves[h]], bank[:], COPY, accum_out=part[:])
+            c_ps.append(bank)
+            c_sum.append(part)
+
+        cs = sb.tile([P, SLOTS], F32, name="cs")
+        ccs = sb.tile([P, SLOTS], F32, name="ccs")
+        u0 = sb.tile([P, 1], F32, name="u0")
+        u1 = sb.tile([P, 1], F32, name="u1")
+        x0 = sb.tile([P, 5], F32, name="x0")
+        x1 = sb.tile([P, 5], F32, name="x1")
+        x2 = sb.tile([P, 5], F32, name="x2")
+        lo, hi = halves
+        nc.vector.scalar_tensor_tensor(cs[:, lo], c_sb[:, lo], inv[:], sq[:, lo], MULT, MULT, accum_out=u0[:])
+        nc.vector.scalar_tensor_tensor(ccs[:, lo], c_sb[:, lo], -2.0, cs[:, lo], MULT, MULT, accum_out=sums[:, 1, 0:1])
+        nc.vector.tensor_scalar(x0[:], coef_c, c_sum[0][:], None, MULT)
+        nc.vector.scalar_tensor_tensor(x1[:], coef_u[:], u0[:], x0[:], MULT, ADD)
+        nc.vector.scalar_tensor_tensor(cs[:, hi], c_sb[:, hi], inv[:], sq[:, hi], MULT, MULT, accum_out=u1[:])
+        nc.vector.scalar_tensor_tensor(x2[:], coef_c, c_sum[1][:], x1[:], MULT, ADD)
+        nc.vector.scalar_tensor_tensor(sums[:, 0, :], coef_u[:], u1[:], x2[:], MULT, ADD)
+        nc.vector.scalar_tensor_tensor(ccs[:, hi], c_sb[:, hi], -2.0, cs[:, hi], MULT, MULT, accum_out=sums[:, 1, 1:2])
+        terms = sb.tile([P, 2, 2], F32, name="terms")
+        shift = sb.tile([P, 1], F32, name="shift")
+        nc.vector.scalar_tensor_tensor(terms[:], sums[:, :, 0:2], 1.0, sums[:, :, 2:4], MULT, MULT, accum_out=shift[:])
+
+        dev2 = sb.tile([P, SLOTS], F32, name="dev2")
+        grad = sb.tile([P, SLOTS], F32, name="grad")
+        result = sb.tile([P, SLOTS], F32, name="result")
+        for h in range(2):
+            nc.scalar.activation(dev2[:, halves[h]], c_ps[h][:], SQUARE, bias=sums[:, 0, 4:5])
+        for h in range(2):
+            nc.vector.scalar_tensor_tensor(grad[:, halves[h]], dev2[:, halves[h]], shift[:], score[:, halves[h]], ADD, MULT)
+        for h in range(2):
+            nc.vector.scalar_tensor_tensor(result[:, halves[h]], grad[:, halves[h]], gain[:], base_sb[:, halves[h]], MULT, ADD)
+            queue = nc.sync if h == 0 else nc.scalar
+            queue.dma_start(out=out[:, halves[h]], in_=result[:, halves[h]])

@@ -52,33 +52,33 @@ def tile_attend_gpsquareshares_kernel(
 
         offsets = sb.tile([P, SLOTS // LIST_ROWS], U16, name="offsets")
         key_plane = sb.tile([P, T], U8, name="key_plane", align_bytes=64)
-        val_plane = sb.tile([P, T], U8, name="val_plane", align_bytes=64)
         key_pool = sb.tile([P, T], U16, name="key_pool", align_bytes=64)
         late = ctx.enter_context(tc.tile_pool(name="late", bufs=1))
-        seed = late.tile([P, 1552], F32, name="seed", offset=0)
+        seed = late.tile([P, 2080], F32, name="seed", offset=0)
         coef_u = sb.tile([P, 5], F32, name="coef_u")
 
         nc.vector.memset(key_plane[:].bitcast(I32), 0)
         nc.vector.memset(seed[:, 0:1], 1.0)
         nc.vector.memset(seed[:, 1:5], 0.0)
         nc.vector.tensor_copy(coef_u[:], seed[:, 0:5])
+        val_plane = late.tile([P, T], U8, name="val_plane", offset=8256)
         nc.vector.memset(val_plane[:].bitcast(I32), 0)
 
         q_raw = late.tile([P, PACK, Q], F32, name="q_raw", offset=0)
         val_pool = late.tile([P, T], U16, name="val_pool", offset=2048)
         g_raw = late.tile([P, PACK, Q], F32, name="g_raw", offset=6144)
-        floor_sb = sb.tile([P, 1], F32, name="floor_sb")
-        reserve_sb = sb.tile([P, 1], F32, name="reserve_sb")
+        floor_sb = late.tile([P, 1], F32, name="floor_sb", offset=8192)
+        reserve_sb = late.tile([P, 1], F32, name="reserve_sb", offset=8224)
 
         nc.sync.dma_start(offsets[:], offs)
         nc.sync.dma_start(out=key_pool[:].bitcast(I32), in_=keys_words[0].bitcast(I32))
         load_scale_rows(nc.sync, key_plane, keys_scales)
         nc.sync.dma_start(out=q_raw[:], in_=query.rearrange("(p t) q -> p t q", t=PACK))
+        nc.sync.dma_start(out=g_raw[:], in_=gout.rearrange("(p t) q -> p t q", t=PACK))
         nc.sync.dma_start(out=val_pool[:].bitcast(I32), in_=vals_words[0].bitcast(I32))
         load_scale_rows(nc.sync, val_plane, vals_scales)
-        nc.sync.dma_start(out=g_raw[:], in_=gout.rearrange("(p t) q -> p t q", t=PACK))
-        nc.gpsimd.dma_start(out=floor_sb[:], in_=floor)
-        nc.gpsimd.dma_start(out=reserve_sb[:], in_=reserve)
+        nc.sync.dma_start(out=floor_sb[:], in_=floor)
+        nc.sync.dma_start(out=reserve_sb[:], in_=reserve)
 
         order = ctx.enter_context(tc.tile_pool(name="order", bufs=1))
         q_grouped = order.tile([P, Q * PACK], BF16, name="q_grouped", tag="words0", align_bytes=64)
@@ -95,7 +95,7 @@ def tile_attend_gpsquareshares_kernel(
         nc.vector.memset(raw_cols[:, 5:6], 0.0)
         nc.vector.memset(sums[:, 1, 2:4], 1.0)
 
-        rest = sb.tile([P, 1], F32, name="rest")
+        rest = order.tile([P, 1], F32, name="rest", tag="sum0")
         nc.scalar.activation(rest[:], floor_sb[:], IDENT, bias=reserve_sb[:], scale=float(SLOTS))
         nc.scalar.activation(raw_cols[:, 3:4], floor_sb[:], COPY)
         nc.scalar.activation(raw_cols[:, 4:5], floor_sb[:], COPY, scale=2.0)
@@ -145,17 +145,17 @@ def tile_attend_gpsquareshares_kernel(
         c_ps = []
         c_sum = []
         for h in range(2):
-            val_words = order.tile([P, HALF], U16, name="val_words%d" % h, tag=("words0", "g_then_words")[h], align_bytes=64)
+            val_words = order.tile([P, HALF], U16, name="val_words%d" % h, tag=("words0", "total_then_scale")[h], align_bytes=64)
             lo = h * HALF // LIST_ROWS
             nc.vector.tensor_copy(val_words[:], val_pool[:].indirect(offsets[:, lo : lo + HALF // LIST_ROWS]))
-            val_scale = order.tile([P, HALF], U8, name="val_scale%d" % h, tag=("scale0", "total_then_scale")[h], align_bytes=64)
+            val_scale = order.tile([P, HALF], U8, name="val_scale%d" % h, tag=("scale0", "g_then_words")[h], align_bytes=64)
             nc.vector.tensor_copy(val_scale[:], val_plane[:].indirect(offsets[:, lo : lo + HALF // LIST_ROWS]))
             bank = ps.tile([P, HALF], F32, name="c_ps%d" % h)
             nc.tensor.matmul_mx(
                 out=bank[:], lhsT=g_codes[:].bitcast(FP8X4), lhsT_scale=g_scale[:],
                 rhs=val_words[:].bitcast(FP4X4), rhs_scale=val_scale[:], start=True, stop=True,
             )
-            part = sb.tile([P, 1], F32, name="c_sum%d" % h)
+            part = order.tile([P, 1], F32, name="c_sum%d" % h, tag="sum%d" % h)
             nc.scalar.activation(c_sb[:, halves[h]], bank[:], COPY, accum_out=part[:])
             c_ps.append(bank)
             c_sum.append(part)

@@ -28,10 +28,10 @@ SQUARE = mybir.ActivationFunctionType.Square
 
 
 def load_scale_rows(queue, plane, scales):
-    for quad in range(4):
+    for row in range(4):
         queue.dma_start(
-            out=plane[32 * quad : 32 * quad + 4, :].bitcast(I32),
-            in_=scales[0, 4 * quad : 4 * quad + 4, :].bitcast(I32),
+            out=plane[row:P:32, :].bitcast(I32),
+            in_=scales[0, row:16:4, :].bitcast(I32),
         )
 
 
@@ -55,12 +55,13 @@ def tile_attend_gpsquareshares_kernel(
         key_pool = sb.tile([P, T], U16, name="key_pool", align_bytes=64)
         late = ctx.enter_context(tc.tile_pool(name="late", bufs=1))
         seed = late.tile([P, 2080], F32, name="seed", offset=0)
-        coef_u = sb.tile([P, 5], F32, name="coef_u")
+        cols = sb.tile([P, 2, 7], F32, name="cols")
 
         nc.vector.memset(key_plane[:].bitcast(I32), 0)
-        nc.vector.memset(seed[:, 0:1], 1.0)
-        nc.vector.memset(seed[:, 1:5], 0.0)
-        nc.vector.tensor_copy(coef_u[:], seed[:, 0:5])
+        nc.vector.memset(seed[:, 0:8], 0.0)
+        nc.vector.memset(seed[:, 1:2], 0.5)
+        nc.vector.memset(seed[:, 4:5], -0.5)
+        nc.vector.tensor_copy(cols[:, :, 3:7], seed[:, 0:8].rearrange("p (r j) -> p r j", r=2))
         val_plane = late.tile([P, T], U8, name="val_plane", offset=8256)
         nc.vector.memset(val_plane[:].bitcast(I32), 0)
 
@@ -89,19 +90,17 @@ def tile_attend_gpsquareshares_kernel(
         base_sb = late.tile([P, SLOTS], F32, name="base_sb", offset=0)
         nc.sync.dma_start(out=base_sb[:], in_=base)
 
-        raw_cols = sb.tile([P, 7], F32, name="raw_cols")
-        cols = sb.tile([P, 10], F32, name="cols")
-        sums = sb.tile([P, 2, 5], F32, name="sums")
-        nc.vector.memset(raw_cols[:, 5:6], 0.0)
-        nc.vector.memset(sums[:, 1, 2:4], 1.0)
+        raw = sb.tile([P, 2, 3], F32, name="raw")
+        pair = sb.tile([P, 2, SLOTS + 3], F32, name="pair")
+        nc.vector.memset(pair[:, 1, SLOTS : SLOTS + 1], -0.5)
 
-        rest = order.tile([P, 1], F32, name="rest", tag="sum0")
-        nc.scalar.activation(rest[:], floor_sb[:], IDENT, bias=reserve_sb[:], scale=float(SLOTS))
-        nc.scalar.activation(raw_cols[:, 3:4], floor_sb[:], COPY)
-        nc.scalar.activation(raw_cols[:, 4:5], floor_sb[:], COPY, scale=2.0)
-        nc.scalar.activation(raw_cols[:, 6:7], floor_sb[:], COPY, scale=-1.0)
-        nc.scalar.activation(raw_cols[:, 0:1], rest[:], COPY, scale=2.0)
-        nc.scalar.activation(raw_cols[:, 2:3], rest[:], COPY, scale=-1.0)
+        chain = ctx.enter_context(tc.tile_pool(name="chain", bufs=1))
+        rest_tile = chain.tile([P, 16], F32, name="rest_tile", offset=32)
+        rest = rest_tile[:, 0:1]
+        nc.scalar.activation(rest, floor_sb[:], IDENT, bias=reserve_sb[:], scale=float(SLOTS))
+        nc.scalar.activation(raw[:, 1, 1:2], floor_sb[:], COPY)
+        nc.scalar.activation(raw[:, 0, 0:1], rest, COPY, scale=2.0)
+        nc.scalar.activation(raw[:, 0, 2:3], rest, COPY)
 
         key_scale = sb.tile([P, SLOTS], U8, name="key_scale", align_bytes=64)
         key_words = sb.tile([P, SLOTS], U16, name="key_words", align_bytes=64)
@@ -117,9 +116,11 @@ def tile_attend_gpsquareshares_kernel(
             rhs=key_words[:].bitcast(FP4X4), rhs_scale=key_scale[:], start=True, stop=True,
         )
         sq = sb.tile([P, SLOTS], F32, name="sq")
-        nc.scalar.activation(sq[:], score[:], SQUARE, accum_out=raw_cols[:, 1:2])
-        total = order.tile([P, 1], F32, name="total", tag="total_then_scale", align_bytes=64)
-        nc.scalar.activation(total[:], raw_cols[:, 1:2], IDENT, bias=rest[:])
+        nc.scalar.activation(sq[:], score[:], SQUARE, accum_out=raw[:, 0, 1:2])
+        total = sb.tile([P, 1], F32, name="total")
+        nc.scalar.activation(total[:], raw[:, 0, 1:2], IDENT, bias=rest)
+        nc.scalar.activation(raw[:, 1, 0:1], raw[:, 0, 1:2], IDENT, bias=raw[:, 0, 0:1], scale=3.0)
+        nc.scalar.activation(raw[:, 1, 2:3], raw[:, 0, 1:2], IDENT, bias=raw[:, 0, 0:1])
 
         g_codes = sb.tile([P, Q], U32, name="g_codes", align_bytes=64)
         g_scale = sb.tile([P, Q], U8, name="g_scale", align_bytes=64)
@@ -127,25 +128,30 @@ def tile_attend_gpsquareshares_kernel(
 
         inv = sb.tile([P, 1], F32, name="inv")
         nc.vector.reciprocal(inv[:], total[:])
-        nc.scalar.activation(cols[:, 0:7], raw_cols[:], COPY, scale=inv[:])
-        prtau = sb.tile([P, 1], F32, name="prtau")
-        sigma2 = sb.tile([P, 1], F32, name="sigma2")
+        nc.scalar.activation(cols[:, :, 0:3], raw[:], COPY, scale=inv[:])
+        tau = cols[:, 1, 0:1]
+        share = cols[:, 1, 1:2]
+        coef_v = cols[:, 0, 2:7]
+        coef_u = cols[:, 1, 2:7]
+        nc.scalar.activation(cols[:, 0, 5:7], cols[:, 0, 0:2], COPY, scale=tau)
+        nc.scalar.activation(cols[:, 1, 5:6], cols[:, 1, 2:3], COPY, scale=tau, bias=-1.0)
+        coef_c = sb.tile([P, 5], F32, name="coef_c")
+        v0 = sb.tile([P, 1], F32, name="v0")
+        x0 = sb.tile([P, 5], F32, name="x0")
         gain = sb.tile([P, 1], F32, name="gain")
-        nc.scalar.activation(prtau[:], cols[:, 3:4], IDENT, bias=cols[:, 4:5], scale=cols[:, 1:2])
-        nc.scalar.activation(sigma2[:], cols[:, 1:2], SQUARE)
-        nc.scalar.activation(cols[:, 9:10], cols[:, 2:3], COPY, scale=cols[:, 3:4])
-        nc.scalar.activation(coef_u[:, 4:5], cols[:, 2:3], COPY, bias=-1.0)
-        nc.scalar.activation(cols[:, 7:9], cols[:, 0:2], COPY, scale=prtau[:])
-        nc.scalar.activation(coef_u[:, 2:3], sigma2[:], COPY, bias=3.0, scale=-1.0)
-        nc.scalar.activation(gain[:], inv[:], SQUARE, scale=math.sqrt(PENALTY_GAIN))
-        coef_c = cols[:, 5:10]
 
         halves = [slice(h * HALF, (h + 1) * HALF) for h in range(2)]
-        c_sb = sb.tile([P, SLOTS], F32, name="c_sb")
+        c_sb = pair[:, 0, :]
+        cs = pair[:, 1, :]
         c_ps = []
         c_sum = []
         for h in range(2):
-            val_words = order.tile([P, HALF], U16, name="val_words%d" % h, tag=("words0", "total_then_scale")[h], align_bytes=64)
+            if h == 0:
+                val_words = order.tile([P, HALF], U16, name="val_words0", tag="words0", align_bytes=64)
+                part = chain.tile([P, 1], F32, name="c_sum0", offset=32)
+            else:
+                val_words = chain.tile([P, HALF], U16, name="val_words1", offset=64, align_bytes=64)
+                part = chain.tile([P, 1], F32, name="c_sum1", offset=32)
             lo = h * HALF // LIST_ROWS
             nc.vector.tensor_copy(val_words[:], val_pool[:].indirect(offsets[:, lo : lo + HALF // LIST_ROWS]))
             val_scale = order.tile([P, HALF], U8, name="val_scale%d" % h, tag=("scale0", "g_then_words")[h], align_bytes=64)
@@ -155,36 +161,42 @@ def tile_attend_gpsquareshares_kernel(
                 out=bank[:], lhsT=g_codes[:].bitcast(FP8X4), lhsT_scale=g_scale[:],
                 rhs=val_words[:].bitcast(FP4X4), rhs_scale=val_scale[:], start=True, stop=True,
             )
-            part = order.tile([P, 1], F32, name="c_sum%d" % h, tag="sum%d" % h)
             nc.scalar.activation(c_sb[:, halves[h]], bank[:], COPY, accum_out=part[:])
+            if h == 0:
+                nc.scalar.activation(v0[:], part[:], COPY, scale=share)
+                nc.scalar.activation(coef_c[:], coef_v, COPY, scale=share)
+                nc.scalar.activation(x0[:], coef_v, COPY, scale=v0[:])
             c_ps.append(bank)
             c_sum.append(part)
 
-        cs = sb.tile([P, SLOTS], F32, name="cs")
-        ccs = sb.tile([P, SLOTS], F32, name="ccs")
+        ccs = sb.tile([P, SLOTS + 3], F32, name="ccs")
         u0 = sb.tile([P, 1], F32, name="u0")
         u1 = sb.tile([P, 1], F32, name="u1")
-        x0 = sb.tile([P, 5], F32, name="x0")
         x1 = sb.tile([P, 5], F32, name="x1")
         x2 = sb.tile([P, 5], F32, name="x2")
-        lo, hi = halves
-        nc.vector.scalar_tensor_tensor(cs[:, lo], c_sb[:, lo], inv[:], sq[:, lo], MULT, MULT, accum_out=u0[:])
-        nc.vector.scalar_tensor_tensor(ccs[:, lo], c_sb[:, lo], -2.0, cs[:, lo], MULT, MULT, accum_out=sums[:, 1, 0:1])
-        nc.vector.tensor_scalar(x0[:], coef_c, c_sum[0][:], None, MULT)
-        nc.vector.scalar_tensor_tensor(x1[:], coef_u[:], u0[:], x0[:], MULT, ADD)
-        nc.vector.scalar_tensor_tensor(cs[:, hi], c_sb[:, hi], inv[:], sq[:, hi], MULT, MULT, accum_out=u1[:])
-        nc.vector.scalar_tensor_tensor(x2[:], coef_c, c_sum[1][:], x1[:], MULT, ADD)
-        nc.vector.scalar_tensor_tensor(sums[:, 0, :], coef_u[:], u1[:], x2[:], MULT, ADD)
-        nc.vector.scalar_tensor_tensor(ccs[:, hi], c_sb[:, hi], -2.0, cs[:, hi], MULT, MULT, accum_out=sums[:, 1, 1:2])
-        terms = sb.tile([P, 2, 2], F32, name="terms")
+        centre = sb.tile([P, 1], F32, name="centre")
         shift = sb.tile([P, 1], F32, name="shift")
-        nc.vector.scalar_tensor_tensor(terms[:], sums[:, :, 0:2], 1.0, sums[:, :, 2:4], MULT, MULT, accum_out=shift[:])
+        lo, hi = halves
+        tail = slice(HALF, SLOTS + 3)
+        nc.vector.scalar_tensor_tensor(cs[:, lo], c_sb[:, lo], inv[:], sq[:, lo], MULT, MULT, accum_out=u0[:])
+        nc.vector.scalar_tensor_tensor(ccs[:, lo], c_sb[:, lo], -2.0, cs[:, lo], MULT, MULT, accum_out=c_sb[:, SLOTS : SLOTS + 1])
+        nc.vector.scalar_tensor_tensor(x1[:], coef_u, u0[:], x0[:], MULT, ADD)
+        nc.vector.scalar_tensor_tensor(cs[:, hi], c_sb[:, hi], inv[:], sq[:, hi], MULT, MULT, accum_out=u1[:])
+        nc.vector.scalar_tensor_tensor(x2[:], coef_c[:], c_sum[1][:], x1[:], MULT, ADD)
+        nc.vector.scalar_tensor_tensor(
+            pair[:, :, SLOTS + 1 : SLOTS + 3],
+            coef_u[:, 1:5].rearrange("p (r j) -> p r j", r=2), u1[:],
+            x2[:, 1:5].rearrange("p (r j) -> p r j", r=2), MULT, ADD,
+        )
+        nc.scalar.activation(centre[:], u1[:], IDENT, bias=x2[:, 0:1], scale=coef_u[:, 0:1])
+        nc.vector.scalar_tensor_tensor(ccs[:, tail], c_sb[:, tail], -2.0, cs[:, tail], MULT, MULT, accum_out=shift[:])
 
         dev2 = sb.tile([P, SLOTS], F32, name="dev2")
         grad = sb.tile([P, SLOTS], F32, name="grad")
         result = sb.tile([P, SLOTS], F32, name="result")
         for h in range(2):
-            nc.scalar.activation(dev2[:, halves[h]], c_ps[h][:], SQUARE, bias=sums[:, 0, 4:5])
+            nc.scalar.activation(dev2[:, halves[h]], c_ps[h][:], SQUARE, bias=centre[:], scale=-1.0)
+        nc.scalar.activation(gain[:], inv[:], SQUARE, scale=math.sqrt(PENALTY_GAIN))
         for h in range(2):
             nc.vector.scalar_tensor_tensor(grad[:, halves[h]], dev2[:, halves[h]], shift[:], score[:, halves[h]], ADD, MULT)
         for h in range(2):

import math
from contextlib import ExitStack

import concourse.mybir as mybir

D, E, T, SLOTS, Q = 512, 512, 2048, 512, 128
P = 128
PACK = 4
HALF = SLOTS // 2
LIST_ROWS = 16
PENALTY_GAIN = 4.0 * 512.0 * 2.0 * 512.0

FLOPS = 2 * Q * SLOTS * (D + E)

F32 = mybir.dt.float32
BF16 = mybir.dt.bfloat16
I32 = mybir.dt.int32
U32 = mybir.dt.uint32
U16 = mybir.dt.uint16
U8 = mybir.dt.uint8
FP8X4 = mybir.dt.float8_e4m3fn_x4
FP4X4 = mybir.dt.float4_e2m1fn_x4
MULT = mybir.AluOpType.mult
ADD = mybir.AluOpType.add
COPY = mybir.ActivationFunctionType.Copy
IDENT = mybir.ActivationFunctionType.Identity
SQUARE = mybir.ActivationFunctionType.Square


def load_scale_rows(queue, plane, scales):
    for row in range(4):
        queue.dma_start(
            out=plane[row:P:32, :].bitcast(I32),
            in_=scales[0, row:16:4, :].bitcast(I32),
        )


def interleave(nc, grouped, raw):
    nc.scalar.copy(
        out=grouped[:].rearrange("p (c i t) -> p c t i", i=4, t=PACK),
        in_=raw[:].rearrange("p t (c i) -> p c t i", i=4),
    )


def tile_attend_gpsquareshares_kernel(
    tc, query, keys_words, keys_scales, floor, reserve, gout, vals_words, vals_scales, base, offs, out
):
    nc = tc.nc
    with ExitStack() as ctx:
        sb = ctx.enter_context(tc.tile_pool(name="sb", bufs=1))
        ps = ctx.enter_context(tc.psum_pool(name="ps", bufs=1))

        offsets = sb.tile([P, SLOTS // LIST_ROWS], U16, name="offsets")
        key_plane = sb.tile([P, T], U8, name="key_plane", align_bytes=64)
        key_pool = sb.tile([P, T], U16, name="key_pool", align_bytes=64)
        late = ctx.enter_context(tc.tile_pool(name="late", bufs=1))
        seed = late.tile([P, 2080], F32, name="seed", offset=0)
        cols = sb.tile([P, 2, 7], F32, name="cols")

        nc.vector.memset(key_plane[:].bitcast(I32), 0)
        nc.vector.memset(seed[:, 0:8], 0.0)
        nc.vector.memset(seed[:, 1:2], 0.5)
        nc.vector.memset(seed[:, 4:5], -0.5)
        nc.vector.tensor_copy(cols[:, :, 3:7], seed[:, 0:8].rearrange("p (r j) -> p r j", r=2))
        val_plane = late.tile([P, T], U8, name="val_plane", offset=8256)
        nc.vector.memset(val_plane[:].bitcast(I32), 0)

        q_raw = late.tile([P, PACK, Q], F32, name="q_raw", offset=0)
        val_pool = late.tile([P, T], U16, name="val_pool", offset=2048)
        g_raw = late.tile([P, PACK, Q], F32, name="g_raw", offset=6144)
        floor_sb = late.tile([P, 1], F32, name="floor_sb", offset=8192)
        reserve_sb = late.tile([P, 1], F32, name="reserve_sb", offset=8224)

        nc.sync.dma_start(offsets[:], offs)
        nc.sync.dma_start(out=key_pool[:].bitcast(I32), in_=keys_words[0].bitcast(I32))
        load_scale_rows(nc.sync, key_plane, keys_scales)
        nc.sync.dma_start(out=q_raw[:], in_=query.rearrange("(p t) q -> p t q", t=PACK))
        nc.sync.dma_start(out=g_raw[:], in_=gout.rearrange("(p t) q -> p t q", t=PACK))
        nc.sync.dma_start(out=val_pool[:].bitcast(I32), in_=vals_words[0].bitcast(I32))
        load_scale_rows(nc.sync, val_plane, vals_scales)
        nc.sync.dma_start(out=floor_sb[:], in_=floor)
        nc.sync.dma_start(out=reserve_sb[:], in_=reserve)

        order = ctx.enter_context(tc.tile_pool(name="order", bufs=1))
        q_grouped = order.tile([P, Q * PACK], BF16, name="q_grouped", tag="words0", align_bytes=64)
        g_grouped = order.tile([P, Q * PACK], BF16, name="g_grouped", tag="g_then_words", align_bytes=64)
        interleave(nc, q_grouped, q_raw)
        interleave(nc, g_grouped, g_raw)

        base_sb = late.tile([P, SLOTS], F32, name="base_sb", offset=0)
        nc.sync.dma_start(out=base_sb[:], in_=base)

        raw = sb.tile([P, 2, 3], F32, name="raw")
        pair = sb.tile([P, 2, SLOTS + 3], F32, name="pair")
        nc.vector.memset(pair[:, 1, SLOTS : SLOTS + 1], -0.5)

        chain = ctx.enter_context(tc.tile_pool(name="chain", bufs=1))
        rest_tile = chain.tile([P, 16], F32, name="rest_tile", offset=32)
        rest = rest_tile[:, 0:1]
        nc.scalar.activation(rest, floor_sb[:], IDENT, bias=reserve_sb[:], scale=float(SLOTS))
        nc.scalar.activation(raw[:, 1, 1:2], floor_sb[:], COPY)
        nc.scalar.activation(raw[:, 0, 0:1], rest, COPY, scale=2.0)
        nc.scalar.activation(raw[:, 0, 2:3], rest, COPY)

        key_scale = sb.tile([P, SLOTS], U8, name="key_scale", align_bytes=64)
        key_words = sb.tile([P, SLOTS], U16, name="key_words", align_bytes=64)
        nc.vector.tensor_copy(key_words[:], key_pool[:].indirect(offsets[:]))
        nc.vector.tensor_copy(key_scale[:], key_plane[:].indirect(offsets[:]))
        q_codes = sb.tile([P, Q], U32, name="q_codes", align_bytes=64)
        q_scale = sb.tile([P, Q], U8, name="q_scale", align_bytes=64)
        nc.vector.quantize_mx(out=q_codes[:].bitcast(FP8X4), scales=q_scale[:], in_=q_grouped[:])

        score = ps.tile([P, SLOTS], F32, name="score")
        nc.tensor.matmul_mx(
            out=score[:], lhsT=q_codes[:].bitcast(FP8X4), lhsT_scale=q_scale[:],
            rhs=key_words[:].bitcast(FP4X4), rhs_scale=key_scale[:], start=True, stop=True,
        )
        sq = sb.tile([P, SLOTS], F32, name="sq")
        nc.scalar.activation(sq[:], score[:], SQUARE, accum_out=raw[:, 0, 1:2])
        total = sb.tile([P, 1], F32, name="total")
        nc.scalar.activation(total[:], raw[:, 0, 1:2], IDENT, bias=rest)
        nc.scalar.activation(raw[:, 1, 0:1], raw[:, 0, 1:2], IDENT, bias=raw[:, 0, 0:1], scale=3.0)
        nc.scalar.activation(raw[:, 1, 2:3], raw[:, 0, 1:2], IDENT, bias=raw[:, 0, 0:1])

        g_codes = sb.tile([P, Q], U32, name="g_codes", align_bytes=64)
        g_scale = sb.tile([P, Q], U8, name="g_scale", align_bytes=64)
        nc.vector.quantize_mx(out=g_codes[:].bitcast(FP8X4), scales=g_scale[:], in_=g_grouped[:])

        inv = sb.tile([P, 1], F32, name="inv")
        nc.vector.reciprocal(inv[:], total[:])
        nc.scalar.activation(cols[:, :, 0:3], raw[:], COPY, scale=inv[:])
        tau = cols[:, 1, 0:1]
        share = cols[:, 1, 1:2]
        coef_v = cols[:, 0, 2:7]
        coef_u = cols[:, 1, 2:7]
        nc.scalar.activation(cols[:, 0, 5:7], cols[:, 0, 0:2], COPY, scale=tau)
        nc.scalar.activation(cols[:, 1, 5:6], cols[:, 1, 2:3], COPY, scale=tau, bias=-1.0)
        coef_c = sb.tile([P, 5], F32, name="coef_c")
        v0 = sb.tile([P, 1], F32, name="v0")
        x0 = sb.tile([P, 5], F32, name="x0")
        gain = sb.tile([P, 1], F32, name="gain")

        halves = [slice(h * HALF, (h + 1) * HALF) for h in range(2)]
        c_sb = pair[:, 0, :]
        cs = pair[:, 1, :]
        c_ps = []
        c_sum = []
        for h in range(2):
            if h == 0:
                val_words = order.tile([P, HALF], U16, name="val_words0", tag="words0", align_bytes=64)
                part = chain.tile([P, 1], F32, name="c_sum0", offset=32)
            else:
                val_words = chain.tile([P, HALF], U16, name="val_words1", offset=64, align_bytes=64)
                part = chain.tile([P, 1], F32, name="c_sum1", offset=32)
            lo = h * HALF // LIST_ROWS
            nc.vector.tensor_copy(val_words[:], val_pool[:].indirect(offsets[:, lo : lo + HALF // LIST_ROWS]))
            val_scale = order.tile([P, HALF], U8, name="val_scale%d" % h, tag=("scale0", "g_then_words")[h], align_bytes=64)
            nc.vector.tensor_copy(val_scale[:], val_plane[:].indirect(offsets[:, lo : lo + HALF // LIST_ROWS]))
            bank = ps.tile([P, HALF], F32, name="c_ps%d" % h)
            nc.tensor.matmul_mx(
                out=bank[:], lhsT=g_codes[:].bitcast(FP8X4), lhsT_scale=g_scale[:],
                rhs=val_words[:].bitcast(FP4X4), rhs_scale=val_scale[:], start=True, stop=True,
            )
            nc.scalar.activation(c_sb[:, halves[h]], bank[:], COPY, accum_out=part[:])
            if h == 0:
                nc.scalar.activation(v0[:], part[:], COPY, scale=share)
                nc.scalar.activation(coef_c[:], coef_v, COPY, scale=share)
                nc.scalar.activation(x0[:], coef_v, COPY, scale=v0[:])
            c_ps.append(bank)
            c_sum.append(part)

        ccs = sb.tile([P, SLOTS + 3], F32, name="ccs")
        u0 = sb.tile([P, 1], F32, name="u0")
        u1 = sb.tile([P, 1], F32, name="u1")
        x1 = sb.tile([P, 5], F32, name="x1")
        x2 = sb.tile([P, 5], F32, name="x2")
        centre = sb.tile([P, 1], F32, name="centre")
        shift = sb.tile([P, 1], F32, name="shift")
        lo, hi = halves
        tail = slice(HALF, SLOTS + 3)
        nc.vector.scalar_tensor_tensor(cs[:, lo], c_sb[:, lo], inv[:], sq[:, lo], MULT, MULT, accum_out=u0[:])
        nc.vector.scalar_tensor_tensor(ccs[:, lo], c_sb[:, lo], -2.0, cs[:, lo], MULT, MULT, accum_out=c_sb[:, SLOTS : SLOTS + 1])
        nc.vector.scalar_tensor_tensor(x1[:], coef_u, u0[:], x0[:], MULT, ADD)
        nc.vector.scalar_tensor_tensor(cs[:, hi], c_sb[:, hi], inv[:], sq[:, hi], MULT, MULT, accum_out=u1[:])
        nc.vector.scalar_tensor_tensor(x2[:], coef_c[:], c_sum[1][:], x1[:], MULT, ADD)
        nc.vector.scalar_tensor_tensor(
            pair[:, :, SLOTS + 1 : SLOTS + 3],
            coef_u[:, 1:5].rearrange("p (r j) -> p r j", r=2), u1[:],
            x2[:, 1:5].rearrange("p (r j) -> p r j", r=2), MULT, ADD,
        )
        nc.scalar.activation(centre[:], u1[:], IDENT, bias=x2[:, 0:1], scale=coef_u[:, 0:1])
        nc.vector.scalar_tensor_tensor(ccs[:, tail], c_sb[:, tail], -2.0, cs[:, tail], MULT, MULT, accum_out=shift[:])

        dev2 = sb.tile([P, SLOTS], F32, name="dev2")
        grad = sb.tile([P, SLOTS], F32, name="grad")
        result = sb.tile([P, SLOTS], F32, name="result")
        for h in range(2):
            nc.scalar.activation(dev2[:, halves[h]], c_ps[h][:], SQUARE, bias=centre[:], scale=-1.0)
        nc.scalar.activation(gain[:], inv[:], SQUARE, scale=math.sqrt(PENALTY_GAIN))
        for h in range(2):
            nc.vector.scalar_tensor_tensor(grad[:, halves[h]], dev2[:, halves[h]], shift[:], score[:, halves[h]], ADD, MULT)
        for h in range(2):
            nc.vector.scalar_tensor_tensor(result[:, halves[h]], grad[:, halves[h]], gain[:], base_sb[:, halves[h]], MULT, ADD)
            queue = nc.sync if h == 0 else nc.scalar
            queue.dma_start(out=out[:, halves[h]], in_=result[:, halves[h]])
